import numpy as np, ml_dtypes
CORES = [23,119,17,113]
N = 4
import mx_ref
BF = ml_dtypes.bfloat16
def entries(a):
    return np.ascontiguousarray(a.T).reshape(-1)
def table(e):
    return np.ascontiguousarray(np.reshape(e, (-1, 16)).T).astype(np.int32)
def cols(t, e):
    v = np.concatenate([t.reshape(128, -1, 4), np.zeros((128, 1, 4), BF)], axis=1)
    return np.ascontiguousarray(v[:, e]).reshape(128, -1)
def tile(rs):
    return np.stack(rs, axis=2).reshape(128, -1).astype(BF)
def cut(t, i, w=512):
    return t[:, w * i:w * i + w]
def rowtile(v, k):
    z = np.concatenate([v, np.zeros((1, v.shape[1]), BF)])
    return np.concatenate([np.ascontiguousarray(z[k[:, 4 * m:4 * m + 4]].transpose(0, 2, 1)).reshape(128, -1) for m in range(k.shape[1] // 4)], axis=1)
def f(rng, *shape):
    return mx_ref.flush((rng.standard_normal(shape, dtype=np.float32) * np.exp2(rng.integers(-2, 3, shape[:-1] + (1,)))).astype(BF))
def wide(rng, *shape, cols=0):
    v = rng.standard_normal(shape, dtype=np.float32) * np.exp2(rng.integers(-12, 13, shape)).astype(np.float32)
    if cols: v *= np.repeat(np.exp2(rng.integers(-cols, cols + 1, shape[:-2] + (1, shape[-1] // 4))) * (rng.random(shape[:-2] + (1, shape[-1] // 4)) > 0.0625), 4, axis=-1).astype(np.float32)
    return mx_ref.flush(v.astype(BF))
T, HU, ACT = 256, 1536, 512
def lists(rng, how=None):
    a = []
    for r in range(N):
        e = rng.permutation(HU)[:ACT]
        if how == "reversed": e = np.sort(e)[::-1]
        if how == "clustered": e = rng.integers(0, HU - ACT + 1) + np.arange(ACT)
        a.append(e)
    return {"act": np.stack([e.reshape(128, 4).astype(np.int32) for e in a]), "actc": np.stack([table(e) for e in a])}
def setup_inputs(rng):
    return {"x": f(rng, N, 128, 4 * T), "w1": f(rng, N, 128, 4 * HU), "w2": f(rng, N, HU, 512), **lists(rng)}
def setup_inputs_clustered(rng):
    return {**setup_inputs(rng), **lists(rng, "clustered")}
def setup_inputs_dead(rng):
    d = setup_inputs(rng); d["x"] = np.abs(d["x"])
    for r in range(N):
        k = d["act"][r].reshape(-1)[rng.permutation(ACT)[:ACT // 2]]
        w = d["w1"][r].reshape(128, HU, 4)
        w[:, k] = -np.abs(w[:, k])
        d["w1"][r] = w.reshape(128, -1)
    return d
def setup_inputs_giant(rng):
    d = setup_inputs(rng)
    for r in range(N):
        k = d["act"][r].reshape(-1)[rng.permutation(ACT)[:ACT // 32]]
        d["w2"][r, k] = (d["w2"][r, k].astype(np.float32) * np.float32(4096)).astype(BF)
    return d
def setup_inputs_reversed(rng):
    return {**setup_inputs(rng), **lists(rng, "reversed")}
def setup_inputs_spread(rng):
    d = setup_inputs(rng); d["x"] = wide(rng, N, 128, 4 * T); d["w2"] = wide(rng, N, HU, 512); return d
def check_inputs(d):
    b = []
    for r in range(N):
        e = d["act"][r].reshape(-1)
        if e.min() < 0 or e.max() >= HU or len(set(e.tolist())) != ACT: b.append("act")
        if (entries(d["actc"][r]) != e).any(): b.append("actc")
    return b
def reference(x, w1, w2, act, actc):
    y = np.zeros((N, 128, 4 * T), np.float32)
    X = [mx_ref.quantize(x[r]) for r in range(N)]
    for s in range(N):
        A = [mx_ref.quantize(cols(w1[s], act[s][:, b])) for b in range(4)]
        rows = rowtile(w2[s], act[s])
        B = [mx_ref.quantize(np.ascontiguousarray(cut(rows, o))) for o in range(4)]
        for r in range(N):
            H = mx_ref.quantize(tile([np.maximum(mx_ref.matmul(A[b], X[r]), np.float32(0)) * np.float32(0.05) for b in range(4)]))
            for o in range(4): y[r][:, T * o:T * o + T] += mx_ref.matmul(B[o], H)
    return {"y": y}

@@ -1,0 +1,292 @@
+from concourse.bass import DstId, RemoteDMATransfer, IndirectOffsetOnAxis
+from concourse.mybir import dt, AluOpType, ActivationFunctionType
+
+F8 = "float8_e4m3fn_x4"
+SCRATCH = {
+    "idx": ("sbuf", [128, 4], "int32"),
+    "lst": ("sbuf", [128, 64], "int32"),
+    "lf": ("sbuf", [128, 128], "float32"),
+    "lt": ("sbuf", [128, 128], "float32"),
+    "off0": ("sbuf", [128, 128], "uint16"),
+    "off1": ("sbuf", [128, 128], "uint16"),
+    "off2": ("sbuf", [128, 128], "uint16"),
+    "off3": ("sbuf", [128, 128], "uint16"),
+    "xs": ("sbuf", [128, 1024], "bfloat16"),
+    "ws": ("sbuf", [128, 6144], "bfloat16"),
+    "at": ("sbuf", [128, 2048], "bfloat16"),
+    "aq": ("sbuf", [128, 512], F8),
+    "ap": ("sbuf", [128, 512], "uint8"),
+    "rw": ("sbuf", [128, 2048], "bfloat16"),
+    "bt": ("sbuf", [128, 2048], "bfloat16"),
+    "bq": ("sbuf", [128, 512], F8),
+    "bp": ("sbuf", [128, 512], "uint8"),
+    "xq": ("sbuf", [128, 1024], F8),
+    "xp": ("sbuf", [128, 1024], "uint8"),
+    "ht": ("sbuf", [128, 4096], "bfloat16"),
+    "hq": ("sbuf", [128, 1024], F8),
+    "hp": ("sbuf", [128, 1024], "uint8"),
+    "hl": ("sbuf", [128, 768], F8),
+    "hm": ("sbuf", [128, 768], "uint8"),
+    "bl": ("sbuf", [128, 1536], F8),
+    "bm": ("sbuf", [128, 1536], "uint8"),
+    "ys": ("sbuf", [128, 1024], "float32"),
+    "ps": ("psum", [128, 4096], "float32"),
+}
+SEMAPHORES = (["fill", "actl", "lstl", "xl", "wl", "xqd", "cp", "tr", "ofs", "bcp", "bc0", "bc1", "qb0", "qb1",
+               "eo", "ef", "en", "ho", "hf", "hn", "sent", "yo"]
+              + ["%s%d" % (n, i) for n in ("ga", "qa", "rw", "mo", "mf", "mn", "ym", "ye") for i in range(4)]
+              + ["%s%d" % (n, i) for n in ("ax", "ah", "ab", "ac") for i in range(4)])
+RELU = ActivationFunctionType.Relu
+COPY = ActivationFunctionType.Copy
+
+
+def bits(es):
+    return sum(1 << e for e in es)
+
+
+def rank_program(g, core, T, topo):
+    me = T.rank_of(core)
+    if me is None:
+        return
+    cores = T.cores
+    sem = T.sem
+
+    def slots(r):
+        c = cores[r]
+        off = [s for s in range(4) if topo.chip(cores[s]) != topo.chip(c)]
+        off.sort(key=lambda s: topo.die(cores[s]) != topo.die(c))
+        near = [s for s in range(4) if s != r and topo.chip(cores[s]) == topo.chip(c)]
+        return off + near + [r]
+
+    mine = slots(me)
+    fa, fb, nb = mine[0], mine[1], mine[2]
+
+    def slot_at(r):
+        return slots(r).index(me)
+
+    def dst(r):
+        rid, pid, _ = topo.addr(cores[r])
+        return DstId(rid=rid, pnc=pid)
+
+    far_e = topo.engines(core, cores[fa])
+    rest = [e for e in topo.engines(core, cores[nb]) if e not in far_e]
+    near_e = rest[::2]
+    far, near = bits(far_e), bits(near_e)
+    half = len(far_e) // 2
+    far_lo, far_hi = bits(far_e[:half]), bits(far_e[half:])
+    nhalf = len(near_e) // 2
+    near_b, near_h = bits(near_e[:nhalf]), bits([e for e in rest if e not in near_e][:nhalf])
+    NF, NN = len(far_e), len(near_e)
+    sent = [0]
+
+    def codes(buf, a, b):
+        return T[buf][:, a:b].bitcast(dt.uint8)
+
+    def plane(buf, a, b):
+        return T[buf][:, a:b]
+
+    def move(mask, s, src, pairs):
+        sent[0] += sum(mask >> e & 1 for e in range(16))
+        return RemoteDMATransfer(dst_ids=[dst(r) for r, _ in pairs], dma_engine_mask=mask, remote_sem=sem[s],
+                                 srcs=[src], dsts=[d for _, d in pairs])
+
+    def send(ts):
+        g.remote_dma_fused(ts, local_sem=sem.sent)
+
+    V, S, P, Y = g.vector, g.scalar, g.tensor, g.sync
+
+    S.dma_start(T.idx[:], T.act[:]).then_inc(sem.actl, 16)
+    Y.dma_start(T.xs[:], T.x[:]).then_inc(sem.xl, 16)
+    V.memset(T.lst[:], 0).then_inc(sem.fill, 1)
+    S.wait_ge(sem.fill, 1)
+    for k in range(4):
+        S.dma_start(T.lst[32 * k:32 * k + 8, :], T.act[:]).then_inc(sem.lstl, 16)
+    Y.dma_start(T.ws[:, 0:3072], T.w1[:, 0:3072]).then_inc(sem.wl, 16)
+    S.dma_start(T.ws[:, 3072:6144], T.w1[:, 3072:6144]).then_inc(sem.wl, 16)
+
+    def rows(t):
+        g.indirect_dma_start(T.rw[:, 512 * t:512 * t + 512], None, T.w2[:],
+                             IndirectOffsetOnAxis(ap=T.idx[:, t:t + 1], axis=0),
+                             bounds_check=1535).then_inc(sem["rw%d" % t], 16)
+
+    def own(r, w):
+        k = slot_at(r)
+        return w * k, w * k + w
+
+    g.wait_ge(sem.actl, 16)
+    rows(0)
+    g.wait_ge(sem.xqd, 1)
+    ax = "ax%d" % me
+    send([move(far, ax, codes("xq", 768, 1024), [(r, codes("xq", *own(r, 256))) for r in (fa, fb)]),
+          move(near, ax, codes("xq", 768, 1024), [(nb, codes("xq", *own(nb, 256)))])])
+    send([move(far, ax, plane("xp", 768, 1024), [(r, plane("xp", *own(r, 256))) for r in (fa, fb)]),
+          move(near, ax, plane("xp", 768, 1024), [(nb, plane("xp", *own(nb, 256)))])])
+    for t in range(1, 4):
+        rows(t)
+    ah, ab, ac = "ah%d" % me, "ab%d" % me, "ac%d" % me
+    g.wait_ge(sem.hf, 1)
+    send([move(far_lo, ah, codes("hq", 0, 256), [(fa, codes("hl", *own(fa, 256)))]),
+          move(far_hi, ah, codes("hq", 256, 512), [(fb, codes("hl", *own(fb, 256)))])])
+    send([move(far_lo, ah, plane("hp", 0, 256), [(fa, plane("hm", *own(fa, 256)))]),
+          move(far_hi, ah, plane("hp", 256, 512), [(fb, plane("hm", *own(fb, 256)))])])
+
+    def bcol(r, a, b):
+        k = 512 * slot_at(r)
+        return k + a, k + b
+
+    g.wait_ge(sem.qb0, 1)
+    send([move(far, ab, codes("bq", 0, 256), [(r, codes("bl", *bcol(r, 0, 256))) for r in (fa, fb)]),
+          move(near, ab, codes("bq", 0, 256), [(nb, codes("bl", *bcol(nb, 0, 256)))])])
+    g.wait_ge(sem.qb1, 1)
+    send([move(far, ab, plane("bp", 0, 512), [(r, plane("bm", *bcol(r, 0, 512))) for r in (fa, fb)]),
+          move(near, ab, plane("bp", 0, 512), [(nb, plane("bm", *bcol(nb, 0, 512)))])])
+    g.wait_ge(sem.hn, 1)
+    send([move(far, ac, codes("bq", 256, 512), [(r, codes("bl", *bcol(r, 256, 512))) for r in (fa, fb)]),
+          move(near_b, ac, codes("bq", 256, 512), [(nb, codes("bl", *bcol(nb, 256, 512)))]),
+          move(near_h, ah, codes("hq", 512, 768), [(nb, codes("hl", *own(nb, 256)))])])
+    send([move(near_h, ah, plane("hp", 512, 768), [(nb, plane("hm", *own(nb, 256)))])])
+    g.wait_ge(sem.sent, sent[0])
+
+    V.wait_ge(sem.xl, 16)
+    V.quantize_mx(T.xq[:, 768:1024], T.xp[:, 768:1024], T.xs[:]).then_inc(sem.xqd, 1)
+    V.wait_ge(sem.lstl, 64)
+    for b in range(4):
+        for d in range(2):
+            a = 32 * b + 16 * d
+            V.tensor_copy(T.lf[:, a:a + 16], T.lst[:, b:64:4]).then_inc(sem.cp, 1)
+    V.wait_ge(sem.cp, 8)
+    V.transpose(T.lt[:], T.lf[:]).then_inc(sem.tr, 1)
+    V.wait_ge(sem.tr, 1)
+    for t in range(4):
+        V.tensor_scalar(T["off%d" % t][:], T.lt[:], 4.0, float(t), AluOpType.mult, AluOpType.add).then_inc(sem.ofs, 1)
+
+    def tile_cols(b, t):
+        return T.at[:, 512 * b + t:512 * b + 512:4]
+
+    def listed(b, t):
+        return T.ws[:, 0:6144].indirect(T["off%d" % t][:, 32 * b:32 * b + 8])
+
+    def quant_a(b):
+        V.wait_ge(sem["ga%d" % b], 4)
+        V.quantize_mx(T.aq[:, 128 * b:128 * b + 128], T.ap[:, 128 * b:128 * b + 128],
+                      T.at[:, 512 * b:512 * b + 512]).then_inc(sem["qa%d" % b], 1)
+
+    V.wait_ge(sem.ofs, 4)
+    V.wait_ge(sem.wl, 32)
+    S.wait_ge(sem.ofs, 4)
+    S.wait_ge(sem.wl, 32)
+    for b in range(4):
+        for t in range(2):
+            V.tensor_copy(tile_cols(b, t), listed(b, t)).then_inc(sem["ga%d" % b], 1)
+            S.activation(tile_cols(b, t + 2), listed(b, t + 2), COPY).then_inc(sem["ga%d" % b], 1)
+        if b:
+            quant_a(b - 1)
+    quant_a(3)
+
+    def relu_s(b, bank, n, base, done, s):
+        S.wait_ge(sem[done], 1)
+        S.activation(T.ht[:, base + b:base + 4 * n:4], T.ps[:, 512 * bank:512 * bank + n], RELU,
+                     scale=0.05).then_inc(sem[s], 1)
+
+    def relu_v(b, bank, n, base, done, s):
+        V.wait_ge(sem[done], 1)
+        V.tensor_scalar(T.ht[:, base + b:base + 4 * n:4], T.ps[:, 512 * bank:512 * bank + n], 0.0, 0.05,
+                        AluOpType.max, AluOpType.mult).then_inc(sem[s], 1)
+
+    for b in range(4):
+        relu_s(b, 4 + b, 256, 3072, "mo%d" % b, "eo")
+    relu_s(0, 0, 512, 0, "mf0", "ef")
+    relu_s(2, 2, 512, 0, "mf2", "ef")
+    for b in range(4):
+        relu_s(b, 4 + b, 256, 2048, "mn%d" % b, "en")
+
+    def inter(t, a, b, s):
+        V.tensor_copy(T.bt[:, 4 * a + t:4 * b:4], T.rw[:, 512 * t + a:512 * t + b]).then_inc(sem[s], 1)
+
+    for t in range(2):
+        V.wait_ge(sem["rw%d" % t], 16)
+        inter(t, 0, 512, "bcp")
+    relu_v(1, 1, 512, 0, "mf1", "ef")
+    relu_v(3, 3, 512, 0, "mf3", "ef")
+    V.wait_ge(sem.ef, 4)
+    V.quantize_mx(T.hq[:, 0:512], T.hp[:, 0:512], T.ht[:, 0:2048]).then_inc(sem.hf, 1)
+    V.wait_ge(sem.eo, 4)
+    V.quantize_mx(T.hq[:, 768:1024], T.hp[:, 768:1024], T.ht[:, 3072:4096]).then_inc(sem.ho, 1)
+    V.wait_ge(sem.rw2, 16)
+    inter(2, 0, 512, "bcp")
+    V.wait_ge(sem.rw3, 16)
+    inter(3, 0, 256, "bc0")
+    inter(3, 256, 512, "bc1")
+    V.wait_ge(sem.bcp, 3)
+    V.wait_ge(sem.bc0, 1)
+    V.quantize_mx(T.bq[:, 0:256], T.bp[:, 0:256], T.bt[:, 0:1024]).then_inc(sem.qb0, 1)
+    V.wait_ge(sem.bc1, 1)
+    V.quantize_mx(T.bq[:, 256:512], T.bp[:, 256:512], T.bt[:, 1024:2048]).then_inc(sem.qb1, 1)
+    V.wait_ge(sem.en, 4)
+    V.quantize_mx(T.hq[:, 512:768], T.hp[:, 512:768], T.ht[:, 2048:3072]).then_inc(sem.hn, 1)
+
+    def layer1(b, a, n, bank, s):
+        P.matmul_mx(T.ps[:, 512 * bank:512 * bank + n], T.aq[:, 128 * b:128 * b + 128], T.ap[:, 128 * b:128 * b + 128],
+                    T.xq[:, a:a + n], T.xp[:, a:a + n], True, True).then_inc(sem[s], 1)
+
+    P.wait_ge(sem.xqd, 1)
+    for b in range(4):
+        P.wait_ge(sem["qa%d" % b], 1)
+        layer1(b, 768, 256, 4 + b, "mo%d" % b)
+    P.wait_ge(sem["ax%d" % fa], 2 * NF)
+    P.wait_ge(sem["ax%d" % fb], 2 * NF)
+    for b in range(4):
+        layer1(b, 0, 512, b, "mf%d" % b)
+    P.wait_ge(sem["ax%d" % nb], 2 * NN)
+    P.wait_ge(sem.eo, 4)
+    for b in range(4):
+        layer1(b, 512, 256, 4 + b, "mn%d" % b)
+
+    def layer2(o, k, start, stop):
+        if k == 3:
+            w, ws, a, h, hs, c = T.bq, T.bp, 128 * o, T.hq, T.hp, 768
+        else:
+            w, ws, a, h, hs, c = T.bl, T.bm, 512 * k + 128 * o, T.hl, T.hm, 256 * k
+        i = P.matmul_mx(T.ps[:, 512 * o:512 * o + 256], w[:, a:a + 128], ws[:, a:a + 128],
+                        h[:, c:c + 256], hs[:, c:c + 256], start, stop)
+        if stop:
+            i.then_inc(sem["ym%d" % o], 1)
+
+    P.wait_ge(sem.ef, 4)
+    P.wait_ge(sem.ho, 1)
+    P.wait_ge(sem.qb0, 1)
+    layer2(0, 3, True, False)
+    layer2(1, 3, True, False)
+    P.wait_ge(sem.qb1, 1)
+    layer2(2, 3, True, False)
+    layer2(3, 3, True, False)
+    for k, r in ((0, fa), (1, fb)):
+        P.wait_ge(sem["ah%d" % r], 2 * half)
+        P.wait_ge(sem["ab%d" % r], 2 * NF)
+        layer2(0, k, False, False)
+        layer2(1, k, False, False)
+    P.wait_ge(sem["ab%d" % nb], 2 * NN)
+    P.wait_ge(sem["ah%d" % nb], 2 * nhalf)
+    layer2(0, 2, False, True)
+    layer2(1, 2, False, True)
+    P.wait_ge(sem["ac%d" % nb], nhalf)
+    layer2(2, 2, False, False)
+    layer2(3, 2, False, False)
+    P.wait_ge(sem["ac%d" % fa], NF)
+    layer2(2, 0, False, False)
+    P.wait_ge(sem["ac%d" % fb], NF)
+    layer2(2, 1, False, True)
+    layer2(3, 0, False, False)
+    layer2(3, 1, False, True)
+
+    for o in range(4):
+        a = 256 * o
+        q = S if o % 2 else V
+        q.wait_ge(sem["ym%d" % o], 1)
+        if o % 2:
+            S.activation(T.ys[:, a:a + 256], T.ps[:, 512 * o:512 * o + 256], COPY).then_inc(sem["ye%d" % o], 1)
+        else:
+            V.tensor_copy(T.ys[:, a:a + 256], T.ps[:, 512 * o:512 * o + 256]).then_inc(sem["ye%d" % o], 1)
+        Y.wait_ge(sem["ye%d" % o], 1)
+        Y.dma_start(T.y[:, a:a + 256], T.ys[:, a:a + 256]).then_inc(sem.yo, 16)
+    Y.wait_ge(sem.yo, 64)

@@ -1,6 +1,7 @@
 from concourse.bass import DstId, RemoteDMATransfer, IndirectOffsetOnAxis
 from concourse.mybir import dt, AluOpType, ActivationFunctionType
 
+CUT = 256
 F8 = "float8_e4m3fn_x4"
 SCRATCH = {
     "idx": ("sbuf", [128, 4], "int32"),
@@ -12,6 +13,8 @@ SCRATCH = {
     "off2": ("sbuf", [128, 128], "uint16"),
     "off3": ("sbuf", [128, 128], "uint16"),
     "xs": ("sbuf", [128, 1024], "bfloat16"),
+    "xq": ("sbuf", [128, 256], F8),
+    "xp": ("sbuf", [128, 256], "uint8"),
     "ws": ("sbuf", [128, 6144], "bfloat16"),
     "at": ("sbuf", [128, 2048], "bfloat16"),
     "aq": ("sbuf", [128, 512], F8),
@@ -20,28 +23,23 @@ SCRATCH = {
     "bt": ("sbuf", [128, 2048], "bfloat16"),
     "bq": ("sbuf", [128, 512], F8),
     "bp": ("sbuf", [128, 512], "uint8"),
-    "xq": ("sbuf", [128, 1024], F8),
-    "xp": ("sbuf", [128, 1024], "uint8"),
+    "al": ("sbuf", [128, 1536], F8),
+    "am": ("sbuf", [128, 1536], "uint8"),
+    "bl": ("sbuf", [128, 1536], F8),
+    "bm": ("sbuf", [128, 1536], "uint8"),
     "ht": ("sbuf", [128, 4096], "bfloat16"),
     "hq": ("sbuf", [128, 1024], F8),
     "hp": ("sbuf", [128, 1024], "uint8"),
-    "hl": ("sbuf", [128, 768], F8),
-    "hm": ("sbuf", [128, 768], "uint8"),
-    "bl": ("sbuf", [128, 1536], F8),
-    "bm": ("sbuf", [128, 1536], "uint8"),
     "ys": ("sbuf", [128, 1024], "float32"),
     "ps": ("psum", [128, 4096], "float32"),
 }
 SEMAPHORES = (["fill", "actl", "lstl", "xl", "wl", "xqd", "cp", "tr", "ofs", "bcp", "bc0", "bc1", "qb0", "qb1",
-               "eo", "ef", "en", "ho", "hf", "hn", "sent", "yo"]
-              + ["%s%d" % (n, i) for n in ("ga", "qa", "rw", "mo", "mf", "mn", "ym", "ye") for i in range(4)]
-              + ["%s%d" % (n, i) for n in ("ax", "ah", "ab", "ac") for i in range(4)])
+               "sent", "yo"]
+              + ["%s%d" % (n, i) for n in ("ga", "qa", "rw", "ym", "ye", "qh", "aa", "as", "ar", "ab", "ac")
+                 for i in range(4)]
+              + ["%s%d%d" % (n, k, b) for n in "me" for k in range(4) for b in range(4)])
 RELU = ActivationFunctionType.Relu
 COPY = ActivationFunctionType.Copy
-
-
-def bits(es):
-    return sum(1 << e for e in es)
 
 
 def rank_program(g, core, T, topo):
@@ -58,25 +56,17 @@ def rank_program(g, core, T, topo):
         near = [s for s in range(4) if s != r and topo.chip(cores[s]) == topo.chip(c)]
         return off + near + [r]
 
-    mine = slots(me)
-    fa, fb, nb = mine[0], mine[1], mine[2]
-
-    def slot_at(r):
-        return slots(r).index(me)
+    fa, fb, nb, _ = slots(me)
 
     def dst(r):
         rid, pid, _ = topo.addr(cores[r])
         return DstId(rid=rid, pnc=pid)
 
     far_e = topo.engines(core, cores[fa])
-    rest = [e for e in topo.engines(core, cores[nb]) if e not in far_e]
-    near_e = rest[::2]
-    far, near = bits(far_e), bits(near_e)
+    near_e = [e for e in topo.engines(core, cores[nb]) if e not in far_e]
+    even_e, odd_e = near_e[::2], near_e[1::2]
     half = len(far_e) // 2
-    far_lo, far_hi = bits(far_e[:half]), bits(far_e[half:])
-    nhalf = len(near_e) // 2
-    near_b, near_h = bits(near_e[:nhalf]), bits([e for e in rest if e not in near_e][:nhalf])
-    NF, NN = len(far_e), len(near_e)
+    lo_e, hi_e = far_e[:half], far_e[half:]
     sent = [0]
 
     def codes(buf, a, b):
@@ -85,70 +75,51 @@ def rank_program(g, core, T, topo):
     def plane(buf, a, b):
         return T[buf][:, a:b]
 
-    def move(mask, s, src, pairs):
-        sent[0] += sum(mask >> e & 1 for e in range(16))
-        return RemoteDMATransfer(dst_ids=[dst(r) for r, _ in pairs], dma_engine_mask=mask, remote_sem=sem[s],
-                                 srcs=[src], dsts=[d for _, d in pairs])
+    def move(es, s, f, src, to, a, b, rs):
+        sent[0] += len(es)
+        at = [512 * slots(r).index(me) for r in rs]
+        return RemoteDMATransfer(dst_ids=[dst(r) for r in rs], dma_engine_mask=sum(1 << e for e in es),
+                                 remote_sem=sem[s], srcs=[f(src, a, b)], dsts=[f(to, k + a, k + b) for k in at])
 
     def send(ts):
         g.remote_dma_fused(ts, local_sem=sem.sent)
 
     V, S, P, Y = g.vector, g.scalar, g.tensor, g.sync
 
-    S.dma_start(T.idx[:], T.act[:]).then_inc(sem.actl, 16)
-    Y.dma_start(T.xs[:], T.x[:]).then_inc(sem.xl, 16)
+    Y.dma_start(T.idx[:], T.act[:]).then_inc(sem.actl, 16)
     V.memset(T.lst[:], 0).then_inc(sem.fill, 1)
     S.wait_ge(sem.fill, 1)
     for k in range(4):
         S.dma_start(T.lst[32 * k:32 * k + 8, :], T.act[:]).then_inc(sem.lstl, 16)
     Y.dma_start(T.ws[:, 0:3072], T.w1[:, 0:3072]).then_inc(sem.wl, 16)
     S.dma_start(T.ws[:, 3072:6144], T.w1[:, 3072:6144]).then_inc(sem.wl, 16)
+    Y.dma_start(T.xs[:], T.x[:]).then_inc(sem.xl, 16)
 
-    def rows(t):
+    g.wait_ge(sem.actl, 16)
+    for t in range(4):
         g.indirect_dma_start(T.rw[:, 512 * t:512 * t + 512], None, T.w2[:],
                              IndirectOffsetOnAxis(ap=T.idx[:, t:t + 1], axis=0),
                              bounds_check=1535).then_inc(sem["rw%d" % t], 16)
-
-    def own(r, w):
-        k = slot_at(r)
-        return w * k, w * k + w
-
-    g.wait_ge(sem.actl, 16)
-    rows(0)
-    g.wait_ge(sem.xqd, 1)
-    ax = "ax%d" % me
-    send([move(far, ax, codes("xq", 768, 1024), [(r, codes("xq", *own(r, 256))) for r in (fa, fb)]),
-          move(near, ax, codes("xq", 768, 1024), [(nb, codes("xq", *own(nb, 256)))])])
-    send([move(far, ax, plane("xp", 768, 1024), [(r, plane("xp", *own(r, 256))) for r in (fa, fb)]),
-          move(near, ax, plane("xp", 768, 1024), [(nb, plane("xp", *own(nb, 256)))])])
-    for t in range(1, 4):
-        rows(t)
-    ah, ab, ac = "ah%d" % me, "ab%d" % me, "ac%d" % me
-    g.wait_ge(sem.hf, 1)
-    send([move(far_lo, ah, codes("hq", 0, 256), [(fa, codes("hl", *own(fa, 256)))]),
-          move(far_hi, ah, codes("hq", 256, 512), [(fb, codes("hl", *own(fb, 256)))])])
-    send([move(far_lo, ah, plane("hp", 0, 256), [(fa, plane("hm", *own(fa, 256)))]),
-          move(far_hi, ah, plane("hp", 256, 512), [(fb, plane("hm", *own(fb, 256)))])])
-
-    def bcol(r, a, b):
-        k = 512 * slot_at(r)
-        return k + a, k + b
-
+    aa, az, ar, ab, ac = ["%s%d" % (n, me) for n in ("aa", "as", "ar", "ab", "ac")]
+    for b in range(4):
+        g.wait_ge(sem["qa%d" % b], 1)
+    send([move(lo_e, aa, codes, "aq", "al", 0, 256, (fa,)), move(hi_e, aa, codes, "aq", "al", 256, 512, (fb,)),
+          move(even_e, aa, codes, "aq", "al", 0, 256, (nb,)), move(odd_e, aa, codes, "aq", "al", 256, 512, (nb,))])
+    send([move(far_e, az, plane, "ap", "am", 0, 512, (fa, fb)), move(near_e, az, plane, "ap", "am", 0, 512, (nb,))])
     g.wait_ge(sem.qb0, 1)
-    send([move(far, ab, codes("bq", 0, 256), [(r, codes("bl", *bcol(r, 0, 256))) for r in (fa, fb)]),
-          move(near, ab, codes("bq", 0, 256), [(nb, codes("bl", *bcol(nb, 0, 256)))])])
+    send([move(far_e, ab, codes, "bq", "bl", 0, CUT, (fa, fb))])
     g.wait_ge(sem.qb1, 1)
-    send([move(far, ab, plane("bp", 0, 512), [(r, plane("bm", *bcol(r, 0, 512))) for r in (fa, fb)]),
-          move(near, ab, plane("bp", 0, 512), [(nb, plane("bm", *bcol(nb, 0, 512)))])])
-    g.wait_ge(sem.hn, 1)
-    send([move(far, ac, codes("bq", 256, 512), [(r, codes("bl", *bcol(r, 256, 512))) for r in (fa, fb)]),
-          move(near_b, ac, codes("bq", 256, 512), [(nb, codes("bl", *bcol(nb, 256, 512)))]),
-          move(near_h, ah, codes("hq", 512, 768), [(nb, codes("hl", *own(nb, 256)))])])
-    send([move(near_h, ah, plane("hp", 512, 768), [(nb, plane("hm", *own(nb, 256)))])])
+    send([move(far_e, ab, plane, "bp", "bm", 0, 512, (fa, fb)), move(near_e, ab, plane, "bp", "bm", 0, 512, (nb,))])
+    send([move(far_e, ac, codes, "bq", "bl", CUT, 512, (fa, fb))])
+    for r in (fa, fb):
+        g.wait_ge(sem["aa%d" % r], half)
+    sent[0] += len(near_e)
+    send([RemoteDMATransfer(dst_ids=[dst(nb)], dma_engine_mask=sum(1 << e for e in es), remote_sem=sem[ar],
+                            srcs=[codes("al", a, a + 256)], dsts=[codes("al", z, z + 256)])
+          for es, a, z in ((even_e, 0, 512), (odd_e, 768, 256))])
+    send([move(near_e, ac, codes, "bq", "bl", 0, 512, (nb,))])
     g.wait_ge(sem.sent, sent[0])
 
-    V.wait_ge(sem.xl, 16)
-    V.quantize_mx(T.xq[:, 768:1024], T.xp[:, 768:1024], T.xs[:]).then_inc(sem.xqd, 1)
     V.wait_ge(sem.lstl, 64)
     for b in range(4):
         for d in range(2):
@@ -160,133 +131,132 @@ def rank_program(g, core, T, topo):
     for t in range(4):
         V.tensor_scalar(T["off%d" % t][:], T.lt[:], 4.0, float(t), AluOpType.mult, AluOpType.add).then_inc(sem.ofs, 1)
 
-    def tile_cols(b, t):
-        return T.at[:, 512 * b + t:512 * b + 512:4]
-
-    def listed(b, t):
-        return T.ws[:, 0:6144].indirect(T["off%d" % t][:, 32 * b:32 * b + 8])
-
     def quant_a(b):
         V.wait_ge(sem["ga%d" % b], 4)
         V.quantize_mx(T.aq[:, 128 * b:128 * b + 128], T.ap[:, 128 * b:128 * b + 128],
                       T.at[:, 512 * b:512 * b + 512]).then_inc(sem["qa%d" % b], 1)
 
-    V.wait_ge(sem.ofs, 4)
-    V.wait_ge(sem.wl, 32)
-    S.wait_ge(sem.ofs, 4)
-    S.wait_ge(sem.wl, 32)
+    for q in (V, S):
+        q.wait_ge(sem.ofs, 4)
+        q.wait_ge(sem.wl, 32)
     for b in range(4):
-        for t in range(2):
-            V.tensor_copy(tile_cols(b, t), listed(b, t)).then_inc(sem["ga%d" % b], 1)
-            S.activation(tile_cols(b, t + 2), listed(b, t + 2), COPY).then_inc(sem["ga%d" % b], 1)
+        for t in range(4):
+            col = T.at[:, 512 * b + t:512 * b + 512:4]
+            win = T.ws[:, 0:6144].indirect(T["off%d" % t][:, 32 * b:32 * b + 8])
+            if t < (1 if b == 3 else 2):
+                V.tensor_copy(col, win).then_inc(sem["ga%d" % b], 1)
+            else:
+                S.activation(col, win, COPY).then_inc(sem["ga%d" % b], 1)
         if b:
             quant_a(b - 1)
     quant_a(3)
+    V.wait_ge(sem.xl, 16)
+    V.quantize_mx(T.xq[:], T.xp[:], T.xs[:]).then_inc(sem.xqd, 1)
 
-    def relu_s(b, bank, n, base, done, s):
-        S.wait_ge(sem[done], 1)
-        S.activation(T.ht[:, base + b:base + 4 * n:4], T.ps[:, 512 * bank:512 * bank + n], RELU,
-                     scale=0.05).then_inc(sem[s], 1)
+    def relu(q, k, b, bank):
+        q.wait_ge(sem["m%d%d" % (k, b)], 1)
+        out, z = T.ht[:, 1024 * k + b:1024 * k + 1024:4], T.ps[:, 512 * bank:512 * bank + 256]
+        if q is S:
+            i = S.activation(out, z, RELU, scale=0.05)
+        else:
+            i = V.tensor_scalar(out, z, 0.0, 0.05, AluOpType.max, AluOpType.mult)
+        i.then_inc(sem["e%d%d" % (k, b)], 1)
 
-    def relu_v(b, bank, n, base, done, s):
-        V.wait_ge(sem[done], 1)
-        V.tensor_scalar(T.ht[:, base + b:base + 4 * n:4], T.ps[:, 512 * bank:512 * bank + n], 0.0, 0.05,
-                        AluOpType.max, AluOpType.mult).then_inc(sem[s], 1)
-
-    for b in range(4):
-        relu_s(b, 4 + b, 256, 3072, "mo%d" % b, "eo")
-    relu_s(0, 0, 512, 0, "mf0", "ef")
-    relu_s(2, 2, 512, 0, "mf2", "ef")
-    for b in range(4):
-        relu_s(b, 4 + b, 256, 2048, "mn%d" % b, "en")
+    def quant_h(k):
+        for b in range(4):
+            V.wait_ge(sem["e%d%d" % (k, b)], 1)
+        V.quantize_mx(T.hq[:, 256 * k:256 * k + 256], T.hp[:, 256 * k:256 * k + 256],
+                      T.ht[:, 1024 * k:1024 * k + 1024]).then_inc(sem["qh%d" % k], 1)
 
     def inter(t, a, b, s):
         V.tensor_copy(T.bt[:, 4 * a + t:4 * b:4], T.rw[:, 512 * t + a:512 * t + b]).then_inc(sem[s], 1)
 
-    for t in range(2):
+    for k, b, bank in ((3, 0, 0), (3, 2, 2), (2, 0, 0), (2, 2, 2), (0, 1, 1), (1, 3, 3), (0, 3, 1), (1, 1, 3)):
+        relu(S, k, b, bank)
+
+    for t in range(3):
         V.wait_ge(sem["rw%d" % t], 16)
         inter(t, 0, 512, "bcp")
-    relu_v(1, 1, 512, 0, "mf1", "ef")
-    relu_v(3, 3, 512, 0, "mf3", "ef")
-    V.wait_ge(sem.ef, 4)
-    V.quantize_mx(T.hq[:, 0:512], T.hp[:, 0:512], T.ht[:, 0:2048]).then_inc(sem.hf, 1)
-    V.wait_ge(sem.eo, 4)
-    V.quantize_mx(T.hq[:, 768:1024], T.hp[:, 768:1024], T.ht[:, 3072:4096]).then_inc(sem.ho, 1)
-    V.wait_ge(sem.rw2, 16)
-    inter(2, 0, 512, "bcp")
+    for b in (1, 3):
+        relu(V, 3, b, b)
+    quant_h(3)
     V.wait_ge(sem.rw3, 16)
-    inter(3, 0, 256, "bc0")
-    inter(3, 256, 512, "bc1")
+    inter(3, 0, CUT, "bc0")
+    inter(3, CUT, 512, "bc1")
     V.wait_ge(sem.bcp, 3)
     V.wait_ge(sem.bc0, 1)
-    V.quantize_mx(T.bq[:, 0:256], T.bp[:, 0:256], T.bt[:, 0:1024]).then_inc(sem.qb0, 1)
+    V.quantize_mx(T.bq[:, 0:CUT], T.bp[:, 0:CUT], T.bt[:, 0:4 * CUT]).then_inc(sem.qb0, 1)
     V.wait_ge(sem.bc1, 1)
-    V.quantize_mx(T.bq[:, 256:512], T.bp[:, 256:512], T.bt[:, 1024:2048]).then_inc(sem.qb1, 1)
-    V.wait_ge(sem.en, 4)
-    V.quantize_mx(T.hq[:, 512:768], T.hp[:, 512:768], T.ht[:, 2048:3072]).then_inc(sem.hn, 1)
+    V.quantize_mx(T.bq[:, CUT:512], T.bp[:, CUT:512], T.bt[:, 4 * CUT:2048]).then_inc(sem.qb1, 1)
+    for b in (1, 3):
+        relu(V, 2, b, b)
+    quant_h(2)
+    for k, b, bank in ((0, 0, 0), (1, 2, 2), (0, 2, 0), (1, 0, 2)):
+        relu(V, k, b, bank)
+    quant_h(0)
+    quant_h(1)
 
-    def layer1(b, a, n, bank, s):
-        P.matmul_mx(T.ps[:, 512 * bank:512 * bank + n], T.aq[:, 128 * b:128 * b + 128], T.ap[:, 128 * b:128 * b + 128],
-                    T.xq[:, a:a + n], T.xp[:, a:a + n], True, True).then_inc(sem[s], 1)
-
-    P.wait_ge(sem.xqd, 1)
-    for b in range(4):
-        P.wait_ge(sem["qa%d" % b], 1)
-        layer1(b, 768, 256, 4 + b, "mo%d" % b)
-    P.wait_ge(sem["ax%d" % fa], 2 * NF)
-    P.wait_ge(sem["ax%d" % fb], 2 * NF)
-    for b in range(4):
-        layer1(b, 0, 512, b, "mf%d" % b)
-    P.wait_ge(sem["ax%d" % nb], 2 * NN)
-    P.wait_ge(sem.eo, 4)
-    for b in range(4):
-        layer1(b, 512, 256, 4 + b, "mn%d" % b)
+    def layer1(k, b, bank):
+        w, ws, a = (T.aq, T.ap, 128 * b) if k == 3 else (T.al, T.am, 512 * k + 128 * b)
+        P.matmul_mx(T.ps[:, 512 * bank:512 * bank + 256], w[:, a:a + 128], ws[:, a:a + 128],
+                    T.xq[:], T.xp[:], True, True).then_inc(sem["m%d%d" % (k, b)], 1)
 
     def layer2(o, k, start, stop):
-        if k == 3:
-            w, ws, a, h, hs, c = T.bq, T.bp, 128 * o, T.hq, T.hp, 768
-        else:
-            w, ws, a, h, hs, c = T.bl, T.bm, 512 * k + 128 * o, T.hl, T.hm, 256 * k
-        i = P.matmul_mx(T.ps[:, 512 * o:512 * o + 256], w[:, a:a + 128], ws[:, a:a + 128],
-                        h[:, c:c + 256], hs[:, c:c + 256], start, stop)
+        w, ws, a = (T.bq, T.bp, 128 * o) if k == 3 else (T.bl, T.bm, 512 * k + 128 * o)
+        z, c = 2048 + 512 * o, 256 * k
+        i = P.matmul_mx(T.ps[:, z:z + 256], w[:, a:a + 128], ws[:, a:a + 128],
+                        T.hq[:, c:c + 256], T.hp[:, c:c + 256], start, stop)
         if stop:
             i.then_inc(sem["ym%d" % o], 1)
 
-    P.wait_ge(sem.ef, 4)
-    P.wait_ge(sem.ho, 1)
+    K = CUT // 128
+    P.wait_ge(sem.xqd, 1)
+    for b in range(4):
+        P.wait_ge(sem["qa%d" % b], 1)
+        layer1(3, b, b)
+    P.wait_ge(sem.qh3, 1)
     P.wait_ge(sem.qb0, 1)
-    layer2(0, 3, True, False)
-    layer2(1, 3, True, False)
     P.wait_ge(sem.qb1, 1)
-    layer2(2, 3, True, False)
-    layer2(3, 3, True, False)
-    for k, r in ((0, fa), (1, fb)):
-        P.wait_ge(sem["ah%d" % r], 2 * half)
-        P.wait_ge(sem["ab%d" % r], 2 * NF)
-        layer2(0, k, False, False)
-        layer2(1, k, False, False)
-    P.wait_ge(sem["ab%d" % nb], 2 * NN)
-    P.wait_ge(sem["ah%d" % nb], 2 * nhalf)
-    layer2(0, 2, False, True)
-    layer2(1, 2, False, True)
-    P.wait_ge(sem["ac%d" % nb], nhalf)
-    layer2(2, 2, False, False)
-    layer2(3, 2, False, False)
-    P.wait_ge(sem["ac%d" % fa], NF)
-    layer2(2, 0, False, False)
-    P.wait_ge(sem["ac%d" % fb], NF)
-    layer2(2, 1, False, True)
-    layer2(3, 0, False, False)
-    layer2(3, 1, False, True)
+    for o in range(4):
+        layer2(o, 3, True, False)
+    P.wait_ge(sem["aa%d" % nb], len(near_e))
+    P.wait_ge(sem["as%d" % nb], len(near_e))
+    for b in range(4):
+        layer1(2, b, b)
+    for k, r, bs in ((0, fa, (0, 1)), (1, fb, (2, 3))):
+        P.wait_ge(sem["aa%d" % r], half)
+        P.wait_ge(sem["as%d" % r], len(far_e))
+        for b in bs:
+            P.wait_ge(sem["e2%d" % b], 1)
+            layer1(k, b, b)
+    P.wait_ge(sem["ar%d" % nb], len(near_e))
+    for k, b, bank in ((0, 2, 0), (0, 3, 1), (1, 0, 2), (1, 1, 3)):
+        P.wait_ge(sem["e%d%d" % (bank // 2, bank)], 1)
+        layer1(k, b, bank)
+    for k, r in enumerate((fa, fb)):
+        P.wait_ge(sem["qh%d" % k], 1)
+        P.wait_ge(sem["ab%d" % r], 2 * len(far_e))
+        for o in range(K):
+            layer2(o, k, False, False)
+    P.wait_ge(sem.qh2, 1)
+    P.wait_ge(sem["ab%d" % nb], len(near_e))
+    P.wait_ge(sem["ac%d" % nb], len(near_e))
+    for o in range(4):
+        layer2(o, 2, False, o < K)
+    P.wait_ge(sem["ac%d" % fa], len(far_e))
+    P.wait_ge(sem["ac%d" % fb], len(far_e))
+    for o in range(K, 4):
+        layer2(o, 0, False, False)
+        layer2(o, 1, False, True)
 
     for o in range(4):
-        a = 256 * o
+        a, z = 256 * o, 2048 + 512 * o
         q = S if o % 2 else V
         q.wait_ge(sem["ym%d" % o], 1)
         if o % 2:
-            S.activation(T.ys[:, a:a + 256], T.ps[:, 512 * o:512 * o + 256], COPY).then_inc(sem["ye%d" % o], 1)
+            S.activation(T.ys[:, a:a + 256], T.ps[:, z:z + 256], COPY).then_inc(sem["ye%d" % o], 1)
         else:
-            V.tensor_copy(T.ys[:, a:a + 256], T.ps[:, 512 * o:512 * o + 256]).then_inc(sem["ye%d" % o], 1)
+            V.tensor_copy(T.ys[:, a:a + 256], T.ps[:, z:z + 256]).then_inc(sem["ye%d" % o], 1)
         Y.wait_ge(sem["ye%d" % o], 1)
         Y.dma_start(T.y[:, a:a + 256], T.ys[:, a:a + 256]).then_inc(sem.yo, 16)
     Y.wait_ge(sem.yo, 64)

@@ -1,7 +1,7 @@
 from concourse.bass import DstId, RemoteDMATransfer, IndirectOffsetOnAxis
 from concourse.mybir import dt, AluOpType, ActivationFunctionType
 
-CUT = 256
+CUT = 128
 F8 = "float8_e4m3fn_x4"
 SCRATCH = {
     "idx": ("sbuf", [128, 4], "int32"),
@@ -33,9 +33,9 @@ SCRATCH = {
     "ys": ("sbuf", [128, 1024], "float32"),
     "ps": ("psum", [128, 4096], "float32"),
 }
-SEMAPHORES = (["fill", "actl", "lstl", "xl", "wl", "xqd", "cp", "tr", "ofs", "bcp", "bc0", "bc1", "qb0", "qb1",
-               "sent", "yo"]
-              + ["%s%d" % (n, i) for n in ("ga", "qa", "rw", "ym", "ye", "qh", "aa", "as", "ar", "ab", "ac")
+SEMAPHORES = (["fill", "actl", "lstl", "xl", "wl", "wg", "xqd", "cp", "tr", "ofs", "bcp", "bc0", "bc1", "bc2", "qb0",
+               "qb1", "sent", "yo"]
+              + ["%s%d" % (n, i) for n in ("ga", "qa", "rw", "ym", "ye", "qh", "aa", "ax", "as", "ar", "ab", "bs", "ac")
                  for i in range(4)]
               + ["%s%d%d" % (n, k, b) for n in "me" for k in range(4) for b in range(4)])
 RELU = ActivationFunctionType.Relu
@@ -43,9 +43,6 @@ COPY = ActivationFunctionType.Copy
 
 
 def rank_program(g, core, T, topo):
-    me = T.rank_of(core)
-    if me is None:
-        return
     cores = T.cores
     sem = T.sem
 
@@ -56,18 +53,13 @@ def rank_program(g, core, T, topo):
         near = [s for s in range(4) if s != r and topo.chip(cores[s]) == topo.chip(c)]
         return off + near + [r]
 
-    fa, fb, nb, _ = slots(me)
+    def helper(s):
+        c = cores[slots(s)[0]]
+        return [h for h in topo.cores_of(c) if topo.die(h) == topo.die(c) and h not in cores][0]
 
-    def dst(r):
-        rid, pid, _ = topo.addr(cores[r])
+    def dst(c):
+        rid, pid, _ = topo.addr(c)
         return DstId(rid=rid, pnc=pid)
-
-    far_e = topo.engines(core, cores[fa])
-    near_e = [e for e in topo.engines(core, cores[nb]) if e not in far_e]
-    even_e, odd_e = near_e[::2], near_e[1::2]
-    half = len(far_e) // 2
-    lo_e, hi_e = far_e[:half], far_e[half:]
-    sent = [0]
 
     def codes(buf, a, b):
         return T[buf][:, a:b].bitcast(dt.uint8)
@@ -75,11 +67,42 @@ def rank_program(g, core, T, topo):
     def plane(buf, a, b):
         return T[buf][:, a:b]
 
+    me = T.rank_of(core)
+    if me is None:
+        for s in range(4):
+            if helper(s) == core:
+                rs = slots(s)[:2]
+                es = topo.engines(core, cores[rs[0]])[::2]
+                w = len([e for e in topo.engines(cores[s], core)])
+                at = [512 * slots(r).index(s) for r in rs]
+                for name, f, buf, n in (("as", plane, "am", 512), ("ab", codes, "bl", 256)):
+                    one = sem["%s%d" % (name, s)]
+                    g.wait_ge(one, w)
+                    g.remote_dma_fused([RemoteDMATransfer(
+                        dst_ids=[dst(cores[r]) for r in rs], dma_engine_mask=sum(1 << e for e in es), remote_sem=one,
+                        srcs=[f(buf, 0, n)], dsts=[f(buf, k, k + n) for k in at])], local_sem=sem.sent)
+                g.wait_ge(sem.sent, 2 * len(es))
+        return
+
+    fa, fb, nb, _ = slots(me)
+    hc = helper(me)
+
+    far_e = topo.engines(core, cores[fa])
+    near_e = [e for e in topo.engines(core, cores[nb]) if e not in far_e]
+    even_e, odd_e = near_e[::2], near_e[1::2]
+    help_n = len(topo.engines(helper(fa), core)[::2])
+    sent = [0]
+
     def move(es, s, f, src, to, a, b, rs):
         sent[0] += len(es)
         at = [512 * slots(r).index(me) for r in rs]
-        return RemoteDMATransfer(dst_ids=[dst(r) for r in rs], dma_engine_mask=sum(1 << e for e in es),
+        return RemoteDMATransfer(dst_ids=[dst(cores[r]) for r in rs], dma_engine_mask=sum(1 << e for e in es),
                                  remote_sem=sem[s], srcs=[f(src, a, b)], dsts=[f(to, k + a, k + b) for k in at])
+
+    def lend(s, f, src, to, a, b):
+        sent[0] += len(far_e)
+        return RemoteDMATransfer(dst_ids=[dst(hc)], dma_engine_mask=sum(1 << e for e in far_e),
+                                 remote_sem=sem[s], srcs=[f(src, a, b)], dsts=[f(to, a, b)])
 
     def send(ts):
         g.remote_dma_fused(ts, local_sem=sem.sent)
@@ -88,11 +111,12 @@ def rank_program(g, core, T, topo):
 
     Y.dma_start(T.idx[:], T.act[:]).then_inc(sem.actl, 16)
     V.memset(T.lst[:], 0).then_inc(sem.fill, 1)
-    S.wait_ge(sem.fill, 1)
-    for k in range(4):
-        S.dma_start(T.lst[32 * k:32 * k + 8, :], T.act[:]).then_inc(sem.lstl, 16)
-    Y.dma_start(T.ws[:, 0:3072], T.w1[:, 0:3072]).then_inc(sem.wl, 16)
-    S.dma_start(T.ws[:, 3072:6144], T.w1[:, 3072:6144]).then_inc(sem.wl, 16)
+    for q, ks, a in ((Y, (0, 1), 0), (S, (2, 3), 2048)):
+        q.wait_ge(sem.fill, 1)
+        for k in ks:
+            q.dma_start(T.lst[32 * k:32 * k + 8, :], T.act[:]).then_inc(sem.lstl, 16)
+        q.dma_start(T.ws[:, a:a + 2048], T.w1[:, a:a + 2048]).then_inc(sem.wl, 16)
+    g.dma_start(T.ws[:, 4096:6144], T.w1[:, 4096:6144]).then_inc(sem.wg, 16)
     Y.dma_start(T.xs[:], T.x[:]).then_inc(sem.xl, 16)
 
     g.wait_ge(sem.actl, 16)
@@ -100,24 +124,26 @@ def rank_program(g, core, T, topo):
         g.indirect_dma_start(T.rw[:, 512 * t:512 * t + 512], None, T.w2[:],
                              IndirectOffsetOnAxis(ap=T.idx[:, t:t + 1], axis=0),
                              bounds_check=1535).then_inc(sem["rw%d" % t], 16)
-    aa, az, ar, ab, ac = ["%s%d" % (n, me) for n in ("aa", "as", "ar", "ab", "ac")]
-    for b in range(4):
+    aa, ax, az, ar, ab, bz, ac = ["%s%d" % (n, me) for n in ("aa", "ax", "as", "ar", "ab", "bs", "ac")]
+    for b in (0, 1):
         g.wait_ge(sem["qa%d" % b], 1)
-    send([move(lo_e, aa, codes, "aq", "al", 0, 256, (fa,)), move(hi_e, aa, codes, "aq", "al", 256, 512, (fb,)),
-          move(even_e, aa, codes, "aq", "al", 0, 256, (nb,)), move(odd_e, aa, codes, "aq", "al", 256, 512, (nb,))])
-    send([move(far_e, az, plane, "ap", "am", 0, 512, (fa, fb)), move(near_e, az, plane, "ap", "am", 0, 512, (nb,))])
+    send([move(far_e, aa, codes, "aq", "al", 0, 256, (fa,)), move(near_e, aa, codes, "aq", "al", 0, 256, (nb,))])
+    for b in (2, 3):
+        g.wait_ge(sem["qa%d" % b], 1)
+    send([lend(az, plane, "ap", "am", 0, 512), move(near_e, az, plane, "ap", "am", 0, 512, (nb,))])
+    send([move(far_e, ax, codes, "aq", "al", 256, 512, (fb,)), move(near_e, ax, codes, "aq", "al", 256, 512, (nb,))])
     g.wait_ge(sem.qb0, 1)
-    send([move(far_e, ab, codes, "bq", "bl", 0, CUT, (fa, fb))])
+    send([lend(ab, codes, "bq", "bl", 0, 256), move(near_e, ab, codes, "bq", "bl", 0, 256, (nb,))])
     g.wait_ge(sem.qb1, 1)
-    send([move(far_e, ab, plane, "bp", "bm", 0, 512, (fa, fb)), move(near_e, ab, plane, "bp", "bm", 0, 512, (nb,))])
-    send([move(far_e, ac, codes, "bq", "bl", CUT, 512, (fa, fb))])
-    for r in (fa, fb):
-        g.wait_ge(sem["aa%d" % r], half)
+    send([move(far_e, bz, plane, "bp", "bm", 0, 512, (fa, fb)), move(near_e, bz, plane, "bp", "bm", 0, 512, (nb,))])
+    send([move(far_e, ac, codes, "bq", "bl", 256, 512, (fa, fb))])
+    g.wait_ge(sem["aa%d" % fa], len(far_e))
+    g.wait_ge(sem["ax%d" % fb], len(far_e))
     sent[0] += len(near_e)
-    send([RemoteDMATransfer(dst_ids=[dst(nb)], dma_engine_mask=sum(1 << e for e in es), remote_sem=sem[ar],
+    send([RemoteDMATransfer(dst_ids=[dst(cores[nb])], dma_engine_mask=sum(1 << e for e in es), remote_sem=sem[ar],
                             srcs=[codes("al", a, a + 256)], dsts=[codes("al", z, z + 256)])
           for es, a, z in ((even_e, 0, 512), (odd_e, 768, 256))])
-    send([move(near_e, ac, codes, "bq", "bl", 0, 512, (nb,))])
+    send([move(near_e, ac, codes, "bq", "bl", 256, 512, (nb,))])
     g.wait_ge(sem.sent, sent[0])
 
     V.wait_ge(sem.lstl, 64)
@@ -139,6 +165,7 @@ def rank_program(g, core, T, topo):
     for q in (V, S):
         q.wait_ge(sem.ofs, 4)
         q.wait_ge(sem.wl, 32)
+        q.wait_ge(sem.wg, 16)
     for b in range(4):
         for t in range(4):
             col = T.at[:, 512 * b + t:512 * b + 512:4]
@@ -168,26 +195,33 @@ def rank_program(g, core, T, topo):
         V.quantize_mx(T.hq[:, 256 * k:256 * k + 256], T.hp[:, 256 * k:256 * k + 256],
                       T.ht[:, 1024 * k:1024 * k + 1024]).then_inc(sem["qh%d" % k], 1)
 
-    def inter(t, a, b, s):
-        V.tensor_copy(T.bt[:, 4 * a + t:4 * b:4], T.rw[:, 512 * t + a:512 * t + b]).then_inc(sem[s], 1)
+    def inter(q, t, a, b, s):
+        out, rows = T.bt[:, 4 * a + t:4 * b:4], T.rw[:, 512 * t + a:512 * t + b]
+        i = S.activation(out, rows, COPY) if q is S else V.tensor_copy(out, rows)
+        i.then_inc(sem[s], 1)
 
-    for k, b, bank in ((3, 0, 0), (3, 2, 2), (2, 0, 0), (2, 2, 2), (0, 1, 1), (1, 3, 3), (0, 3, 1), (1, 1, 3)):
+    for b in (0, 2):
+        relu(S, 3, b, b)
+    S.wait_ge(sem.rw3, 16)
+    inter(S, 3, CUT, 256, "bc1")
+    inter(S, 3, 256, 512, "bc2")
+    for k, b, bank in ((2, 0, 0), (2, 2, 2), (0, 1, 1), (1, 3, 3), (0, 3, 1), (1, 1, 3)):
         relu(S, k, b, bank)
 
     for t in range(3):
         V.wait_ge(sem["rw%d" % t], 16)
-        inter(t, 0, 512, "bcp")
+        inter(V, t, 0, 512, "bcp")
     for b in (1, 3):
         relu(V, 3, b, b)
     quant_h(3)
     V.wait_ge(sem.rw3, 16)
-    inter(3, 0, CUT, "bc0")
-    inter(3, CUT, 512, "bc1")
+    inter(V, 3, 0, CUT, "bc0")
     V.wait_ge(sem.bcp, 3)
     V.wait_ge(sem.bc0, 1)
-    V.quantize_mx(T.bq[:, 0:CUT], T.bp[:, 0:CUT], T.bt[:, 0:4 * CUT]).then_inc(sem.qb0, 1)
     V.wait_ge(sem.bc1, 1)
-    V.quantize_mx(T.bq[:, CUT:512], T.bp[:, CUT:512], T.bt[:, 4 * CUT:2048]).then_inc(sem.qb1, 1)
+    V.quantize_mx(T.bq[:, 0:256], T.bp[:, 0:256], T.bt[:, 0:1024]).then_inc(sem.qb0, 1)
+    V.wait_ge(sem.bc2, 1)
+    V.quantize_mx(T.bq[:, 256:512], T.bp[:, 256:512], T.bt[:, 1024:2048]).then_inc(sem.qb1, 1)
     for b in (1, 3):
         relu(V, 2, b, b)
     quant_h(2)
@@ -209,7 +243,6 @@ def rank_program(g, core, T, topo):
         if stop:
             i.then_inc(sem["ym%d" % o], 1)
 
-    K = CUT // 128
     P.wait_ge(sem.xqd, 1)
     for b in range(4):
         P.wait_ge(sem["qa%d" % b], 1)
@@ -219,13 +252,13 @@ def rank_program(g, core, T, topo):
     P.wait_ge(sem.qb1, 1)
     for o in range(4):
         layer2(o, 3, True, False)
-    P.wait_ge(sem["aa%d" % nb], len(near_e))
-    P.wait_ge(sem["as%d" % nb], len(near_e))
+    for n in ("aa", "as", "ax"):
+        P.wait_ge(sem["%s%d" % (n, nb)], len(near_e))
     for b in range(4):
         layer1(2, b, b)
-    for k, r, bs in ((0, fa, (0, 1)), (1, fb, (2, 3))):
-        P.wait_ge(sem["aa%d" % r], half)
-        P.wait_ge(sem["as%d" % r], len(far_e))
+    for k, r, n, bs in ((0, fa, "aa", (0, 1)), (1, fb, "ax", (2, 3))):
+        P.wait_ge(sem["%s%d" % (n, r)], len(far_e))
+        P.wait_ge(sem["as%d" % r], help_n)
         for b in bs:
             P.wait_ge(sem["e2%d" % b], 1)
             layer1(k, b, b)
@@ -233,19 +266,23 @@ def rank_program(g, core, T, topo):
     for k, b, bank in ((0, 2, 0), (0, 3, 1), (1, 0, 2), (1, 1, 3)):
         P.wait_ge(sem["e%d%d" % (bank // 2, bank)], 1)
         layer1(k, b, bank)
+    P.wait_ge(sem.qh2, 1)
+    for n in ("ab", "bs"):
+        P.wait_ge(sem["%s%d" % (n, nb)], len(near_e))
+    for o in (0, 1):
+        layer2(o, 2, False, False)
     for k, r in enumerate((fa, fb)):
         P.wait_ge(sem["qh%d" % k], 1)
-        P.wait_ge(sem["ab%d" % r], 2 * len(far_e))
-        for o in range(K):
-            layer2(o, k, False, False)
-    P.wait_ge(sem.qh2, 1)
-    P.wait_ge(sem["ab%d" % nb], len(near_e))
+        P.wait_ge(sem["bs%d" % r], len(far_e))
+        P.wait_ge(sem["ab%d" % r], help_n)
+        for o in (0, 1):
+            layer2(o, k, False, k == 1)
     P.wait_ge(sem["ac%d" % nb], len(near_e))
-    for o in range(4):
-        layer2(o, 2, False, o < K)
+    for o in (2, 3):
+        layer2(o, 2, False, False)
     P.wait_ge(sem["ac%d" % fa], len(far_e))
     P.wait_ge(sem["ac%d" % fb], len(far_e))
-    for o in range(K, 4):
+    for o in (2, 3):
         layer2(o, 0, False, False)
         layer2(o, 1, False, True)
 

from concourse.bass import DstId, RemoteDMATransfer, IndirectOffsetOnAxis
from concourse.mybir import dt, AluOpType, ActivationFunctionType

CUT = 128
F8 = "float8_e4m3fn_x4"
SCRATCH = {
    "idx": ("sbuf", [128, 4], "int32"),
    "lst": ("sbuf", [128, 64], "int32"),
    "lf": ("sbuf", [128, 128], "float32"),
    "lt": ("sbuf", [128, 128], "float32"),
    "off0": ("sbuf", [128, 128], "uint16"),
    "off1": ("sbuf", [128, 128], "uint16"),
    "off2": ("sbuf", [128, 128], "uint16"),
    "off3": ("sbuf", [128, 128], "uint16"),
    "xs": ("sbuf", [128, 1024], "bfloat16"),
    "xq": ("sbuf", [128, 256], F8),
    "xp": ("sbuf", [128, 256], "uint8"),
    "ws": ("sbuf", [128, 6144], "bfloat16"),
    "at": ("sbuf", [128, 2048], "bfloat16"),
    "aq": ("sbuf", [128, 512], F8),
    "ap": ("sbuf", [128, 512], "uint8"),
    "rw": ("sbuf", [128, 2048], "bfloat16"),
    "bt": ("sbuf", [128, 2048], "bfloat16"),
    "bq": ("sbuf", [128, 512], F8),
    "bp": ("sbuf", [128, 512], "uint8"),
    "al": ("sbuf", [128, 1536], F8),
    "am": ("sbuf", [128, 1536], "uint8"),
    "bl": ("sbuf", [128, 1536], F8),
    "bm": ("sbuf", [128, 1536], "uint8"),
    "ht": ("sbuf", [128, 4096], "bfloat16"),
    "hq": ("sbuf", [128, 1024], F8),
    "hp": ("sbuf", [128, 1024], "uint8"),
    "ys": ("sbuf", [128, 1024], "float32"),
    "ps": ("psum", [128, 4096], "float32"),
}
SEMAPHORES = (["fill", "actl", "lstl", "xl", "wl", "wg", "xqd", "cp", "tr", "ofs", "bcp", "bc0", "bc1", "bc2", "qb0",
               "qb1", "sent", "yo"]
              + ["%s%d" % (n, i) for n in ("ga", "qa", "rw", "ym", "ye", "qh", "aa", "ax", "as", "ar", "ab", "bs", "ac")
                 for i in range(4)]
              + ["%s%d%d" % (n, k, b) for n in "me" for k in range(4) for b in range(4)])
RELU = ActivationFunctionType.Relu
COPY = ActivationFunctionType.Copy


def rank_program(g, core, T, topo):
    cores = T.cores
    sem = T.sem

    def slots(r):
        c = cores[r]
        off = [s for s in range(4) if topo.chip(cores[s]) != topo.chip(c)]
        off.sort(key=lambda s: topo.die(cores[s]) != topo.die(c))
        near = [s for s in range(4) if s != r and topo.chip(cores[s]) == topo.chip(c)]
        return off + near + [r]

    def helper(s):
        c = cores[slots(s)[0]]
        return [h for h in topo.cores_of(c) if topo.die(h) == topo.die(c) and h not in cores][0]

    def dst(c):
        rid, pid, _ = topo.addr(c)
        return DstId(rid=rid, pnc=pid)

    def codes(buf, a, b):
        return T[buf][:, a:b].bitcast(dt.uint8)

    def plane(buf, a, b):
        return T[buf][:, a:b]

    me = T.rank_of(core)
    if me is None:
        for s in range(4):
            if helper(s) == core:
                rs = slots(s)[:2]
                es = topo.engines(core, cores[rs[0]])[::2]
                w = len([e for e in topo.engines(cores[s], core)])
                at = [512 * slots(r).index(s) for r in rs]
                for name, f, buf, n in (("as", plane, "am", 512), ("ab", codes, "bl", 256)):
                    one = sem["%s%d" % (name, s)]
                    g.wait_ge(one, w)
                    g.remote_dma_fused([RemoteDMATransfer(
                        dst_ids=[dst(cores[r]) for r in rs], dma_engine_mask=sum(1 << e for e in es), remote_sem=one,
                        srcs=[f(buf, 0, n)], dsts=[f(buf, k, k + n) for k in at])], local_sem=sem.sent)
                g.wait_ge(sem.sent, 2 * len(es))
        return

    fa, fb, nb, _ = slots(me)
    hc = helper(me)

    far_e = topo.engines(core, cores[fa])
    near_e = [e for e in topo.engines(core, cores[nb]) if e not in far_e]
    even_e, odd_e = near_e[::2], near_e[1::2]
    help_n = len(topo.engines(helper(fa), core)[::2])
    sent = [0]

    def move(es, s, f, src, to, a, b, rs):
        sent[0] += len(es)
        at = [512 * slots(r).index(me) for r in rs]
        return RemoteDMATransfer(dst_ids=[dst(cores[r]) for r in rs], dma_engine_mask=sum(1 << e for e in es),
                                 remote_sem=sem[s], srcs=[f(src, a, b)], dsts=[f(to, k + a, k + b) for k in at])

    def lend(s, f, src, to, a, b):
        sent[0] += len(far_e)
        return RemoteDMATransfer(dst_ids=[dst(hc)], dma_engine_mask=sum(1 << e for e in far_e),
                                 remote_sem=sem[s], srcs=[f(src, a, b)], dsts=[f(to, a, b)])

    def send(ts):
        g.remote_dma_fused(ts, local_sem=sem.sent)

    V, S, P, Y = g.vector, g.scalar, g.tensor, g.sync

    Y.dma_start(T.idx[:], T.act[:]).then_inc(sem.actl, 16)
    V.memset(T.lst[:], 0).then_inc(sem.fill, 1)
    for q, ks, a in ((Y, (0, 1), 0), (S, (2, 3), 2048)):
        q.wait_ge(sem.fill, 1)
        for k in ks:
            q.dma_start(T.lst[32 * k:32 * k + 8, :], T.act[:]).then_inc(sem.lstl, 16)
        q.dma_start(T.ws[:, a:a + 2048], T.w1[:, a:a + 2048]).then_inc(sem.wl, 16)
    g.dma_start(T.ws[:, 4096:6144], T.w1[:, 4096:6144]).then_inc(sem.wg, 16)
    Y.dma_start(T.xs[:], T.x[:]).then_inc(sem.xl, 16)

    g.wait_ge(sem.actl, 16)
    for t in range(4):
        g.indirect_dma_start(T.rw[:, 512 * t:512 * t + 512], None, T.w2[:],
                             IndirectOffsetOnAxis(ap=T.idx[:, t:t + 1], axis=0),
                             bounds_check=1535).then_inc(sem["rw%d" % t], 16)
    aa, ax, az, ar, ab, bz, ac = ["%s%d" % (n, me) for n in ("aa", "ax", "as", "ar", "ab", "bs", "ac")]
    for b in (0, 1):
        g.wait_ge(sem["qa%d" % b], 1)
    send([move(far_e, aa, codes, "aq", "al", 0, 256, (fa,)), move(near_e, aa, codes, "aq", "al", 0, 256, (nb,))])
    for b in (2, 3):
        g.wait_ge(sem["qa%d" % b], 1)
    send([lend(az, plane, "ap", "am", 0, 512), move(near_e, az, plane, "ap", "am", 0, 512, (nb,))])
    send([move(far_e, ax, codes, "aq", "al", 256, 512, (fb,)), move(near_e, ax, codes, "aq", "al", 256, 512, (nb,))])
    g.wait_ge(sem.qb0, 1)
    send([lend(ab, codes, "bq", "bl", 0, 256), move(near_e, ab, codes, "bq", "bl", 0, 256, (nb,))])
    g.wait_ge(sem.qb1, 1)
    send([move(far_e, bz, plane, "bp", "bm", 0, 512, (fa, fb)), move(near_e, bz, plane, "bp", "bm", 0, 512, (nb,))])
    send([move(far_e, ac, codes, "bq", "bl", 256, 512, (fa, fb))])
    g.wait_ge(sem["aa%d" % fa], len(far_e))
    g.wait_ge(sem["ax%d" % fb], len(far_e))
    sent[0] += len(near_e)
    send([RemoteDMATransfer(dst_ids=[dst(cores[nb])], dma_engine_mask=sum(1 << e for e in es), remote_sem=sem[ar],
                            srcs=[codes("al", a, a + 256)], dsts=[codes("al", z, z + 256)])
          for es, a, z in ((even_e, 0, 512), (odd_e, 768, 256))])
    send([move(near_e, ac, codes, "bq", "bl", 256, 512, (nb,))])
    g.wait_ge(sem.sent, sent[0])

    V.wait_ge(sem.lstl, 64)
    for b in range(4):
        for d in range(2):
            a = 32 * b + 16 * d
            V.tensor_copy(T.lf[:, a:a + 16], T.lst[:, b:64:4]).then_inc(sem.cp, 1)
    V.wait_ge(sem.cp, 8)
    V.transpose(T.lt[:], T.lf[:]).then_inc(sem.tr, 1)
    V.wait_ge(sem.tr, 1)
    for t in range(4):
        V.tensor_scalar(T["off%d" % t][:], T.lt[:], 4.0, float(t), AluOpType.mult, AluOpType.add).then_inc(sem.ofs, 1)

    def quant_a(b):
        V.wait_ge(sem["ga%d" % b], 4)
        V.quantize_mx(T.aq[:, 128 * b:128 * b + 128], T.ap[:, 128 * b:128 * b + 128],
                      T.at[:, 512 * b:512 * b + 512]).then_inc(sem["qa%d" % b], 1)

    for q in (V, S):
        q.wait_ge(sem.ofs, 4)
        q.wait_ge(sem.wl, 32)
        q.wait_ge(sem.wg, 16)
    for b in range(4):
        for t in range(4):
            col = T.at[:, 512 * b + t:512 * b + 512:4]
            win = T.ws[:, 0:6144].indirect(T["off%d" % t][:, 32 * b:32 * b + 8])
            if t < (1 if b == 3 else 2):
                V.tensor_copy(col, win).then_inc(sem["ga%d" % b], 1)
            else:
                S.activation(col, win, COPY).then_inc(sem["ga%d" % b], 1)
        if b:
            quant_a(b - 1)
    quant_a(3)
    V.wait_ge(sem.xl, 16)
    V.quantize_mx(T.xq[:], T.xp[:], T.xs[:]).then_inc(sem.xqd, 1)

    def relu(q, k, b, bank):
        q.wait_ge(sem["m%d%d" % (k, b)], 1)
        out, z = T.ht[:, 1024 * k + b:1024 * k + 1024:4], T.ps[:, 512 * bank:512 * bank + 256]
        if q is S:
            i = S.activation(out, z, RELU, scale=0.05)
        else:
            i = V.tensor_scalar(out, z, 0.0, 0.05, AluOpType.max, AluOpType.mult)
        i.then_inc(sem["e%d%d" % (k, b)], 1)

    def quant_h(k):
        for b in range(4):
            V.wait_ge(sem["e%d%d" % (k, b)], 1)
        V.quantize_mx(T.hq[:, 256 * k:256 * k + 256], T.hp[:, 256 * k:256 * k + 256],
                      T.ht[:, 1024 * k:1024 * k + 1024]).then_inc(sem["qh%d" % k], 1)

    def inter(q, t, a, b, s):
        out, rows = T.bt[:, 4 * a + t:4 * b:4], T.rw[:, 512 * t + a:512 * t + b]
        i = S.activation(out, rows, COPY) if q is S else V.tensor_copy(out, rows)
        i.then_inc(sem[s], 1)

    for b in (0, 2):
        relu(S, 3, b, b)
    S.wait_ge(sem.rw3, 16)
    inter(S, 3, CUT, 256, "bc1")
    inter(S, 3, 256, 512, "bc2")
    for k, b, bank in ((2, 0, 0), (2, 2, 2), (0, 1, 1), (1, 3, 3), (0, 3, 1), (1, 1, 3)):
        relu(S, k, b, bank)

    for t in range(3):
        V.wait_ge(sem["rw%d" % t], 16)
        inter(V, t, 0, 512, "bcp")
    for b in (1, 3):
        relu(V, 3, b, b)
    quant_h(3)
    V.wait_ge(sem.rw3, 16)
    inter(V, 3, 0, CUT, "bc0")
    V.wait_ge(sem.bcp, 3)
    V.wait_ge(sem.bc0, 1)
    V.wait_ge(sem.bc1, 1)
    V.quantize_mx(T.bq[:, 0:256], T.bp[:, 0:256], T.bt[:, 0:1024]).then_inc(sem.qb0, 1)
    V.wait_ge(sem.bc2, 1)
    V.quantize_mx(T.bq[:, 256:512], T.bp[:, 256:512], T.bt[:, 1024:2048]).then_inc(sem.qb1, 1)
    for b in (1, 3):
        relu(V, 2, b, b)
    quant_h(2)
    for k, b, bank in ((0, 0, 0), (1, 2, 2), (0, 2, 0), (1, 0, 2)):
        relu(V, k, b, bank)
    quant_h(0)
    quant_h(1)

    def layer1(k, b, bank):
        w, ws, a = (T.aq, T.ap, 128 * b) if k == 3 else (T.al, T.am, 512 * k + 128 * b)
        P.matmul_mx(T.ps[:, 512 * bank:512 * bank + 256], w[:, a:a + 128], ws[:, a:a + 128],
                    T.xq[:], T.xp[:], True, True).then_inc(sem["m%d%d" % (k, b)], 1)

    def layer2(o, k, start, stop):
        w, ws, a = (T.bq, T.bp, 128 * o) if k == 3 else (T.bl, T.bm, 512 * k + 128 * o)
        z, c = 2048 + 512 * o, 256 * k
        i = P.matmul_mx(T.ps[:, z:z + 256], w[:, a:a + 128], ws[:, a:a + 128],
                        T.hq[:, c:c + 256], T.hp[:, c:c + 256], start, stop)
        if stop:
            i.then_inc(sem["ym%d" % o], 1)

    P.wait_ge(sem.xqd, 1)
    for b in range(4):
        P.wait_ge(sem["qa%d" % b], 1)
        layer1(3, b, b)
    P.wait_ge(sem.qh3, 1)
    P.wait_ge(sem.qb0, 1)
    P.wait_ge(sem.qb1, 1)
    for o in range(4):
        layer2(o, 3, True, False)
    for n in ("aa", "as", "ax"):
        P.wait_ge(sem["%s%d" % (n, nb)], len(near_e))
    for b in range(4):
        layer1(2, b, b)
    for k, r, n, bs in ((0, fa, "aa", (0, 1)), (1, fb, "ax", (2, 3))):
        P.wait_ge(sem["%s%d" % (n, r)], len(far_e))
        P.wait_ge(sem["as%d" % r], help_n)
        for b in bs:
            P.wait_ge(sem["e2%d" % b], 1)
            layer1(k, b, b)
    P.wait_ge(sem["ar%d" % nb], len(near_e))
    for k, b, bank in ((0, 2, 0), (0, 3, 1), (1, 0, 2), (1, 1, 3)):
        P.wait_ge(sem["e%d%d" % (bank // 2, bank)], 1)
        layer1(k, b, bank)
    P.wait_ge(sem.qh2, 1)
    for n in ("ab", "bs"):
        P.wait_ge(sem["%s%d" % (n, nb)], len(near_e))
    for o in (0, 1):
        layer2(o, 2, False, False)
    for k, r in enumerate((fa, fb)):
        P.wait_ge(sem["qh%d" % k], 1)
        P.wait_ge(sem["bs%d" % r], len(far_e))
        P.wait_ge(sem["ab%d" % r], help_n)
        for o in (0, 1):
            layer2(o, k, False, k == 1)
    P.wait_ge(sem["ac%d" % nb], len(near_e))
    for o in (2, 3):
        layer2(o, 2, False, False)
    P.wait_ge(sem["ac%d" % fa], len(far_e))
    P.wait_ge(sem["ac%d" % fb], len(far_e))
    for o in (2, 3):
        layer2(o, 0, False, False)
        layer2(o, 1, False, True)

    for o in range(4):
        a, z = 256 * o, 2048 + 512 * o
        q = S if o % 2 else V
        q.wait_ge(sem["ym%d" % o], 1)
        if o % 2:
            S.activation(T.ys[:, a:a + 256], T.ps[:, z:z + 256], COPY).then_inc(sem["ye%d" % o], 1)
        else:
            V.tensor_copy(T.ys[:, a:a + 256], T.ps[:, z:z + 256]).then_inc(sem["ye%d" % o], 1)
        Y.wait_ge(sem["ye%d" % o], 1)
        Y.dma_start(T.y[:, a:a + 256], T.ys[:, a:a + 256]).then_inc(sem.yo, 16)
    Y.wait_ge(sem.yo, 64)
